import numpy as np
import ml_dtypes


def mxq(x, axis, fmt="e4m3"):
    dtype, down = {"e4m3": (ml_dtypes.float8_e4m3fn, 7), "e5m2": (ml_dtypes.float8_e5m2, 14)}[fmt]
    v = np.moveaxis(np.asarray(x, np.float32).astype(ml_dtypes.bfloat16).astype(np.float64), axis, -1)
    blocks = v.reshape(v.shape[:-1] + (-1, 32))
    amax = np.abs(blocks).max(-1, keepdims=True)
    byte = np.maximum(np.where(amax > 0, np.frexp(amax)[1] - 1 + 127, 0) - down, 1)
    scale = np.exp2(byte - 127.0)
    codes = (blocks / scale).astype(np.float32).astype(dtype).astype(np.float64)
    return np.moveaxis((codes * scale).reshape(v.shape), -1, axis)


WIDE = False


def mx_kscale(k):
    if not WIDE:
        return np.ones(k)
    levels = np.array([10, -10, 5, -5, 0])
    if k % 512:
        return np.exp2(np.random.permutation(np.resize(levels, k // 32))).repeat(32)
    a = np.empty((k // 512, 16))
    for p in range(k // 512):
        a[p, :8] = np.random.permutation(np.resize(levels, 8))
        for g in range(8):
            far = levels[np.abs(levels - a[p, g]) >= 10]
            a[p, g + 8] = far[np.random.randint(len(far))]
    return np.exp2(a.ravel()).repeat(32)


def f64(x):
    return np.asarray(x).astype(np.float64)


def striped(idx):
    return np.tile(idx.reshape(-1, 16).T, (8, 1)).astype(np.uint16)


def unstriped(offs):
    return offs[:16].T.reshape(-1).astype(np.int64)


def striped8(idx):
    return np.concatenate([x.reshape(-1, 16).T for x in idx]).astype(np.uint16)


def runs(offs, k):
    lists = np.stack([offs[16 * r : 16 * r + 16].T.reshape(-1) for r in range(8)]).astype(np.int64)
    return lists[np.arange(k) % 512 // 64]


def pack_weight(w):
    k, n = w.shape
    w = f64(np.asarray(w, np.float32).astype(ml_dtypes.bfloat16)).reshape(k // 32, 32, n)
    amax = np.abs(w).max(1)
    byte = np.clip(np.where(amax > 0, np.frexp(amax)[1] - 1 + 127 - 7, 1), 1, 254)
    scaled = (w * np.exp2(127.0 - byte)[:, None, :]).reshape(k, n).astype(np.float32)
    words = np.ascontiguousarray(scaled.reshape(k // 512, 128, 4, n).transpose(0, 1, 3, 2)).astype(ml_dtypes.float8_e4m3fn).view(np.uint8)
    return words, np.ascontiguousarray(byte.astype(np.uint8).reshape(k // 512, 16, n))


def unpack_weight(words, scales):
    g, p, n, _ = words.shape
    vals = np.ascontiguousarray(words).view(ml_dtypes.float8_e4m3fn).astype(np.float64) * np.repeat(np.exp2(scales.astype(np.float64) - 127.0), 8, axis=1)[..., None]
    return vals.transpose(0, 1, 3, 2).reshape(g * 512, n)


K, T, S, G, H = 512, 2048, 512, 2048, 512


def setup_inputs():
    n = np.random.standard_normal
    s = mx_kscale(K)[:, None]
    packed_xT = pack_weight(n((K, T)) * s)
    packed_dT = pack_weight(n((K, G)) / s)
    return {
        "x_words": packed_xT[0],
        "x_scales": packed_xT[1],
        "d_words": packed_dT[0],
        "d_scales": packed_dT[1],
        "gs": (np.random.uniform(0.5, 1.5, (K, 1)) * s).astype(np.float32),
        "offs": striped(np.random.permutation(T)[:S]),
        "k1": striped8(np.random.randint(0, G, (8, H))),
        "n1": striped8(np.stack([np.random.permutation(S) for _ in range(8)])),
        "n2": striped8(np.stack([np.random.permutation(S) for _ in range(8)])),
        "k2": striped8(np.random.randint(0, G, (8, H))),
    }


def reference(x_words, x_scales, d_words, d_scales, gs, offs, k1, n1, n2, k2):
    d_k2 = unpack_weight(d_words, d_scales)[np.arange(K)[:, None], runs(k2, K)]
    d_k1 = unpack_weight(d_words, d_scales)[np.arange(K)[:, None], runs(k1, K)]
    xq = unpack_weight(x_words, x_scales)[:, unstriped(offs)]
    h = 0.0625 * (d_k1.T @ xq)
    z = f64(gs) * (h / (np.abs(h[np.arange(H)[:, None], runs(n1, H)]) + np.abs(h[np.arange(H)[:, None], runs(n2, H)]) + 0.5))
    return 0.0625 * ((d_k2.T @ mxq(z, 0, "e4m3")))

@@ -1,0 +1,231 @@
+from contextlib import ExitStack
+
+import concourse.mybir as mybir
+
+K, T, S, G, H = 512, 2048, 512, 2048, 512
+FLOPS = 2 * 2 * K * H * S
+
+F32 = mybir.dt.float32
+BF16 = mybir.dt.bfloat16
+I32 = mybir.dt.int32
+U32 = mybir.dt.uint32
+U16 = mybir.dt.uint16
+U8 = mybir.dt.uint8
+FP8X4 = mybir.dt.float8_e4m3fn_x4
+ACT = mybir.ActivationFunctionType
+ALU = mybir.AluOpType
+
+P = 128
+PACK = 4
+CHUNKS = ((0, 256), (256, 256))
+SCALAR_LOOKS_UP_BOTH = ((1, 1), (1, 2))
+
+
+def tile_picked_pqdiv_none_p_kernel(
+    tc, x_words, x_scales, d_words, d_scales, gs, offs, k1, n1, n2, k2, out
+):
+    nc = tc.nc
+    with ExitStack() as ctx:
+        keep = ctx.enter_context(tc.tile_pool(name="keep", bufs=1))
+        psum = ctx.enter_context(tc.psum_pool(name="psum", bufs=1))
+
+        def load_list(name, src):
+            tile = keep.tile([P, S // 16], U16, name=name)
+            nc.sync.dma_start(tile[:], src)
+            return tile
+
+        def load_words(name, src):
+            tile = keep.tile([P, T], I32, name=name, align_bytes=64)
+            nc.sync.dma_start(tile[:], src[0].rearrange("p c r -> p (c r)").bitcast(I32))
+            return tile
+
+        def gather(name, table, dtype, offsets, tag):
+            tile = keep.tile([P, S], dtype, name=name, tag=tag, align_bytes=64)
+            nc.vector.tensor_copy(tile[:], table[:].bitcast(dtype).indirect(offsets[:]))
+            return tile
+
+        def rows_to_places(plane, queue):
+            words = plane[:].bitcast(I32)
+            for a in range(1, 4):
+                queue.dma_start(words[a:P:32, :], words[8 * a : P : 32, :])
+
+        d_bytes_all = keep.tile([P, G // 4], I32, name="d_bytes_all", align_bytes=64)
+        x_bytes_all = keep.tile([P, T // 4], I32, name="x_bytes_all", align_bytes=64)
+        nc.vector.memset(d_bytes_all[:], 0)
+        nc.gpsimd.memset(x_bytes_all[:], 0)
+        k1_list = load_list("k1_list", k1)
+        nc.sync.dma_start(d_bytes_all[0:P:8, :], d_scales[0].bitcast(I32))
+        offs_list = load_list("offs_list", offs)
+        nc.sync.dma_start(x_bytes_all[0:P:8, :], x_scales[0].bitcast(I32))
+        d_words_all = load_words("d_words_all", d_words)
+        x_words_all = load_words("x_words_all", x_words)
+        gs_sb = keep.tile([P, PACK], F32, name="gs_sb")
+        nc.sync.dma_start(gs_sb[:], gs.rearrange("(p t) o -> p (t o)", t=PACK))
+        n1_list = load_list("n1_list", n1)
+        k2_list = load_list("k2_list", k2)
+        n2_list = load_list("n2_list", n2)
+
+        first_plane = keep.tile([P, H + S], U8, name="first_plane", align_bytes=64)
+        w1_bytes = gather("w1_bytes", d_bytes_all, U8, k1_list, "w1")
+        x_bytes = gather("x_bytes", x_bytes_all, U8, offs_list, "x")
+        nc.vector.tensor_copy(
+            first_plane[:, 0:H].rearrange("p (t m) -> p m t", t=PACK),
+            w1_bytes[:].rearrange("p (m t) -> p m t", t=PACK),
+        )
+        nc.vector.tensor_copy(first_plane[:, H : H + S].bitcast(I32), x_bytes[:].bitcast(I32))
+        rows_to_places(first_plane, nc.sync)
+        w1_picked = gather("w1_picked", d_words_all, U32, k1_list, "w1")
+        w1_dealt = keep.tile([P, H], U32, name="w1_dealt", align_bytes=64)
+        nc.vector.tensor_copy(
+            w1_dealt[:].rearrange("p (t m) -> p m t", t=PACK),
+            w1_picked[:].rearrange("p (m t) -> p m t", t=PACK),
+        )
+        x_picked = keep.tile([P, S], U32, name="x_picked", tag="x", align_bytes=64)
+        h_banks = [psum.tile([P, S], F32, name="h_bank%d" % b) for b in range(PACK)]
+
+        def h_raw(t, tokens):
+            half, start = divmod(tokens.start, S // 2)
+            first = (t % 2) * (S // 2) + start
+            return h_banks[2 * half + t // 2][:, first : first + tokens.stop - tokens.start]
+
+        sizes = [keep.tile([P, S], F32, name="size%d" % t, align_bytes=64) for t in range(PACK)]
+
+        def first_product(t, tokens):
+            cols = slice(P * t, P * (t + 1))
+            nc.tensor.matmul_mx(
+                out=h_raw(t, tokens),
+                lhsT=w1_dealt[:, cols].bitcast(FP8X4),
+                lhsT_scale=first_plane[:, cols],
+                rhs=x_picked[:, tokens].bitcast(FP8X4),
+                rhs_scale=first_plane[:, H + tokens.start : H + tokens.stop],
+                start=True,
+                stop=True,
+            )
+
+        def take_size(t, tokens):
+            nc.scalar.activation(sizes[t][:, tokens], h_raw(t, tokens), ACT.Abs, scale=0.0625)
+
+        halves = (slice(0, S // 2), slice(S // 2, S))
+        for tokens in halves:
+            nc.vector.tensor_copy(
+                x_picked[:, tokens],
+                x_words_all[:].bitcast(U32).indirect(offs_list[:, tokens.start // 16 : tokens.stop // 16]),
+            )
+            for t in range(PACK):
+                first_product(t, tokens)
+        for tokens in halves[:-1]:
+            for t in range(PACK):
+                take_size(t, tokens)
+
+        w2_bytes = gather("w2_bytes", d_bytes_all, U8, k2_list, "w1")
+        second_plane = keep.tile([P, H], U8, name="second_plane", align_bytes=64)
+        nc.vector.tensor_copy(second_plane[:].bitcast(I32), w2_bytes[:].bitcast(I32))
+        rows_to_places(second_plane, nc.sync)
+        w2_picked = gather("w2_picked", d_words_all, U32, k2_list, "w2_picked")
+
+        out_view = out.rearrange("(m p) n -> p m n", p=P)
+        roots = [keep.tile([P, PACK * n], F32, name="roots%d" % c, align_bytes=64) for c, (s0, n) in enumerate(CHUNKS)]
+        half_way = [keep.tile([P, PACK * n], F32, name="half_way%d" % c, align_bytes=64) for c, (s0, n) in enumerate(CHUNKS)]
+        sums = {}
+
+        firsts = {}
+
+        def look_up_first(c, t):
+            s0, n = CHUNKS[c]
+            first = keep.tile([P, n], F32, name="first%d_%d" % (c, t), tag="first", bufs=2, align_bytes=64)
+            nc.scalar.activation(first[:], sizes[t][:].indirect(n1_list[:, s0 // 16 : (s0 + n) // 16]), ACT.Copy)
+            firsts[(c, t)] = first
+
+        def look_up_second(c, t):
+            s0, n = CHUNKS[c]
+            both = keep.tile([P, n], F32, name="both%d_%d" % (c, t), tag="both", bufs=3, align_bytes=64)
+            looked_up = sizes[t][:].indirect(n2_list[:, s0 // 16 : (s0 + n) // 16])
+            if (c, t) in SCALAR_LOOKS_UP_BOTH:
+                second = keep.tile([P, n], F32, name="second%d_%d" % (c, t), align_bytes=64)
+                nc.scalar.activation(second[:], looked_up, ACT.Copy)
+                looked_up = second[:]
+            nc.vector.tensor_tensor(both[:], looked_up, firsts[(c, t)][:], ALU.add)
+            sums[(c, t)] = both
+
+        def take_root(c, t):
+            s0, n = CHUNKS[c]
+            plane = slice(t * n, (t + 1) * n)
+            nc.scalar.activation(roots[c][:, plane], sums[(c, t)][:], ACT.Abs_reciprocal_sqrt, bias=8.0, scale=16.0)
+
+        def weigh(c, t):
+            s0, n = CHUNKS[c]
+            plane = slice(t * n, (t + 1) * n)
+            nc.vector.scalar_tensor_tensor(
+                half_way[c][:, plane],
+                h_raw(t, slice(s0, s0 + n)),
+                gs_sb[:, t : t + 1],
+                roots[c][:, plane],
+                ALU.mult,
+                ALU.mult,
+            )
+
+        def weave(c, lo, hi):
+            n = CHUNKS[c][1]
+            z = keep.tile([P, PACK * (hi - lo)], BF16, name="z%d_%d" % (c, lo), align_bytes=64)
+            nc.vector.tensor_tensor(
+                z[:].rearrange("p (c i t) -> p c t i", i=4, t=PACK),
+                half_way[c][:].rearrange("p (t n) -> p t n", t=PACK)[:, :, lo:hi].rearrange("p t (c i) -> p c t i", i=4),
+                roots[c][:].rearrange("p (t n) -> p t n", t=PACK)[:, :, lo:hi].rearrange("p t (c i) -> p c t i", i=4),
+                ALU.mult,
+            )
+            return z
+
+        def second_product(z, s0, n, last):
+            z_words = keep.tile([P, n], U32, name="z_words%d" % s0, align_bytes=64)
+            z_bytes = keep.tile([P, n], U8, name="z_bytes%d" % s0, align_bytes=64)
+            nc.vector.quantize_mx(out=z_words[:].bitcast(FP8X4), scales=z_bytes[:], in_=z[:])
+            for b in range(2):
+                bank = psum.tile([P, 2 * n], F32, name="out_bank%d_%d" % (s0, b), tag="out_bank", bufs=4)
+                for j in range(2):
+                    cols = slice(P * (2 * b + j), P * (2 * b + j + 1))
+                    nc.tensor.matmul_mx(
+                        out=bank[:, j * n : (j + 1) * n],
+                        lhsT=w2_picked[:, cols].bitcast(FP8X4),
+                        lhsT_scale=second_plane[:, cols],
+                        rhs=z_words[:].bitcast(FP8X4),
+                        rhs_scale=z_bytes[:],
+                        start=True,
+                        stop=True,
+                    )
+                result = keep.tile([P, 2 * n], F32, name="result%d_%d" % (s0, b), align_bytes=64)
+                if b == 1 and last:
+                    nc.vector.tensor_scalar_mul(result[:], bank[:], 0.0625)
+                else:
+                    nc.scalar.activation(result[:], bank[:], ACT.Copy, scale=0.0625)
+                queue = nc.scalar if b == 0 and last else nc.sync
+                queue.dma_start(
+                    out_view[:, 2 * b : 2 * b + 2, s0 : s0 + n],
+                    result[:].rearrange("p (j n) -> p j n", j=2),
+                )
+
+        steps = [(c, t) for c in range(len(CHUNKS)) for t in range(PACK)]
+
+        def at(i):
+            return steps[i : i + 1] if i >= 0 else []
+
+        take_size(0, halves[-1])
+        for i in range(len(steps) + 3):
+            if i + 1 < PACK:
+                take_size(i + 1, halves[-1])
+            for c, t in at(i - 2):
+                take_root(c, t)
+            for c, t in at(i):
+                look_up_first(c, t)
+            for c, t in at(i - 3):
+                weigh(c, t)
+            if i == PACK + 3:
+                second_product(first_z, 0, S // 2, False)
+            for c, t in at(i - 1):
+                look_up_second(c, t)
+            if i == PACK + 2:
+                first_z = weave(0, 0, S // 2)
+        quarter = S // 4
+        third_z = weave(1, 0, quarter)
+        fourth_z = weave(1, quarter, 2 * quarter)
+        second_product(third_z, 2 * quarter, quarter, False)
+        second_product(fourth_z, 3 * quarter, quarter, True)

@@ -65,6 +65,11 @@ def tile_picked_pqdiv_none_p_kernel(
         k2_list = load_list("k2_list", k2)
         n2_list = load_list("n2_list", n2)
 
+        warm_in = keep.tile([P, 1], F32, name="warm_in")
+        nc.gpsimd.memset(warm_in[:], 1.0)
+        warm = keep.tile([P, 1], F32, name="warm")
+        nc.scalar.activation(warm[:], warm_in[:], ACT.Abs_reciprocal_sqrt)
+
         first_plane = keep.tile([P, H + S], U8, name="first_plane", align_bytes=64)
         w1_bytes = gather("w1_bytes", d_bytes_all, U8, k1_list, "w1")
         x_bytes = gather("x_bytes", x_bytes_all, U8, offs_list, "x")

@@ -18,7 +18,8 @@ ALU = mybir.AluOpType
 P = 128
 PACK = 4
 CHUNKS = ((0, 256), (256, 256))
-SCALAR_LOOKS_UP_BOTH = ((1, 1), (1, 2))
+VECTOR_LOOKS_UP_BOTH = ((0, 1),)
+SCALAR_LOOKS_UP_BOTH = ((1, 2), (1, 3))
 
 
 def tile_picked_pqdiv_none_p_kernel(
@@ -34,9 +35,12 @@ def tile_picked_pqdiv_none_p_kernel(
             nc.sync.dma_start(tile[:], src)
             return tile
 
-        def load_words(name, src):
+        def load_words(name, src, pieces):
             tile = keep.tile([P, T], I32, name=name, align_bytes=64)
-            nc.sync.dma_start(tile[:], src[0].rearrange("p c r -> p (c r)").bitcast(I32))
+            words = src[0].rearrange("p c r -> p (c r)").bitcast(I32)
+            for piece in range(pieces):
+                cols = slice(piece * T // pieces, (piece + 1) * T // pieces)
+                nc.sync.dma_start(tile[:, cols], words[:, cols])
             return tile
 
         def gather(name, table, dtype, offsets, tag):
@@ -44,25 +48,24 @@ def tile_picked_pqdiv_none_p_kernel(
             nc.vector.tensor_copy(tile[:], table[:].bitcast(dtype).indirect(offsets[:]))
             return tile
 
-        def rows_to_places(plane, queue):
-            words = plane[:].bitcast(I32)
-            for a in range(1, 4):
-                queue.dma_start(words[a:P:32, :], words[8 * a : P : 32, :])
+        def rows_to_places(plane, source, rows):
+            for a in rows:
+                nc.sync.dma_start(plane[:].bitcast(I32)[a:P:32, :], source[:].bitcast(I32)[8 * a : P : 32, :])
 
         d_bytes_all = keep.tile([P, G // 4], I32, name="d_bytes_all", align_bytes=64)
         x_bytes_all = keep.tile([P, T // 4], I32, name="x_bytes_all", align_bytes=64)
         nc.vector.memset(d_bytes_all[:], 0)
-        nc.gpsimd.memset(x_bytes_all[:], 0)
+        nc.vector.memset(x_bytes_all[:, 0 : T // 8], 0)
+        nc.gpsimd.memset(x_bytes_all[:, T // 8 : T // 4], 0)
         k1_list = load_list("k1_list", k1)
-        nc.sync.dma_start(d_bytes_all[0:P:8, :], d_scales[0].bitcast(I32))
         offs_list = load_list("offs_list", offs)
+        nc.sync.dma_start(d_bytes_all[0:P:8, :], d_scales[0].bitcast(I32))
         nc.sync.dma_start(x_bytes_all[0:P:8, :], x_scales[0].bitcast(I32))
-        d_words_all = load_words("d_words_all", d_words)
-        x_words_all = load_words("x_words_all", x_words)
+        d_words_all = load_words("d_words_all", d_words, 1)
+        x_words_all = load_words("x_words_all", x_words, 2)
         gs_sb = keep.tile([P, PACK], F32, name="gs_sb")
         nc.sync.dma_start(gs_sb[:], gs.rearrange("(p t) o -> p (t o)", t=PACK))
         n1_list = load_list("n1_list", n1)
-        k2_list = load_list("k2_list", k2)
         n2_list = load_list("n2_list", n2)
 
         warm_in = keep.tile([P, 1], F32, name="warm_in")
@@ -74,24 +77,27 @@ def tile_picked_pqdiv_none_p_kernel(
         w1_bytes = gather("w1_bytes", d_bytes_all, U8, k1_list, "w1")
         x_bytes = gather("x_bytes", x_bytes_all, U8, offs_list, "x")
         nc.vector.tensor_copy(
-            first_plane[:, 0:H].rearrange("p (t m) -> p m t", t=PACK),
-            w1_bytes[:].rearrange("p (m t) -> p m t", t=PACK),
+            first_plane[:, 0:H].rearrange("p (t m) -> p t m", t=PACK),
+            w1_bytes[:].rearrange("p (m t) -> p t m", t=PACK),
         )
         nc.vector.tensor_copy(first_plane[:, H : H + S].bitcast(I32), x_bytes[:].bitcast(I32))
-        rows_to_places(first_plane, nc.sync)
+        rows_to_places(first_plane, first_plane, range(1, 4))
+        k2_list = load_list("k2_list", k2)
         w1_picked = gather("w1_picked", d_words_all, U32, k1_list, "w1")
         w1_dealt = keep.tile([P, H], U32, name="w1_dealt", align_bytes=64)
         nc.vector.tensor_copy(
-            w1_dealt[:].rearrange("p (t m) -> p m t", t=PACK),
-            w1_picked[:].rearrange("p (m t) -> p m t", t=PACK),
+            w1_dealt[:].rearrange("p (t c i) -> p c t i", t=PACK, i=4),
+            w1_picked[:].rearrange("p (c i t) -> p c t i", t=PACK, i=4),
         )
         x_picked = keep.tile([P, S], U32, name="x_picked", tag="x", align_bytes=64)
-        h_banks = [psum.tile([P, S], F32, name="h_bank%d" % b) for b in range(PACK)]
+        h_banks = [
+            [psum.tile([P, S // 2], F32, name="h_bank%d_%d" % (half, t), tag="bank%d" % (PACK * half + t)) for t in range(PACK)]
+            for half in range(2)
+        ]
 
         def h_raw(t, tokens):
             half, start = divmod(tokens.start, S // 2)
-            first = (t % 2) * (S // 2) + start
-            return h_banks[2 * half + t // 2][:, first : first + tokens.stop - tokens.start]
+            return h_banks[half][t][:, start : start + tokens.stop - tokens.start]
 
         sizes = [keep.tile([P, S], F32, name="size%d" % t, align_bytes=64) for t in range(PACK)]
 
@@ -116,16 +122,14 @@ def tile_picked_pqdiv_none_p_kernel(
                 x_picked[:, tokens],
                 x_words_all[:].bitcast(U32).indirect(offs_list[:, tokens.start // 16 : tokens.stop // 16]),
             )
-            for t in range(PACK):
-                first_product(t, tokens)
-        for tokens in halves[:-1]:
-            for t in range(PACK):
-                take_size(t, tokens)
+        for pair in range(2):
+            for tokens in halves:
+                for t in (2 * pair, 2 * pair + 1):
+                    first_product(t, tokens)
 
         w2_bytes = gather("w2_bytes", d_bytes_all, U8, k2_list, "w1")
         second_plane = keep.tile([P, H], U8, name="second_plane", align_bytes=64)
-        nc.vector.tensor_copy(second_plane[:].bitcast(I32), w2_bytes[:].bitcast(I32))
-        rows_to_places(second_plane, nc.sync)
+        rows_to_places(second_plane, w2_bytes, range(4))
         w2_picked = gather("w2_picked", d_words_all, U32, k2_list, "w2_picked")
 
         out_view = out.rearrange("(m p) n -> p m n", p=P)
@@ -134,21 +138,29 @@ def tile_picked_pqdiv_none_p_kernel(
         sums = {}
 
         firsts = {}
+        seconds = {}
 
         def look_up_first(c, t):
             s0, n = CHUNKS[c]
-            first = keep.tile([P, n], F32, name="first%d_%d" % (c, t), tag="first", bufs=2, align_bytes=64)
-            nc.scalar.activation(first[:], sizes[t][:].indirect(n1_list[:, s0 // 16 : (s0 + n) // 16]), ACT.Copy)
+            first = keep.tile([P, n], F32, name="first%d_%d" % (c, t), tag="first", bufs=3, align_bytes=64)
+            looked_up = sizes[t][:].indirect(n1_list[:, s0 // 16 : (s0 + n) // 16])
+            if (c, t) in VECTOR_LOOKS_UP_BOTH:
+                nc.vector.tensor_copy(first[:], looked_up)
+            else:
+                nc.scalar.activation(first[:], looked_up, ACT.Copy)
+            if (c, t) in SCALAR_LOOKS_UP_BOTH:
+                second = keep.tile([P, n], F32, name="second%d_%d" % (c, t), align_bytes=64)
+                nc.scalar.activation(second[:], sizes[t][:].indirect(n2_list[:, s0 // 16 : (s0 + n) // 16]), ACT.Copy)
+                seconds[(c, t)] = second
             firsts[(c, t)] = first
 
         def look_up_second(c, t):
             s0, n = CHUNKS[c]
             both = keep.tile([P, n], F32, name="both%d_%d" % (c, t), tag="both", bufs=3, align_bytes=64)
-            looked_up = sizes[t][:].indirect(n2_list[:, s0 // 16 : (s0 + n) // 16])
             if (c, t) in SCALAR_LOOKS_UP_BOTH:
-                second = keep.tile([P, n], F32, name="second%d_%d" % (c, t), align_bytes=64)
-                nc.scalar.activation(second[:], looked_up, ACT.Copy)
-                looked_up = second[:]
+                looked_up = seconds[(c, t)][:]
+            else:
+                looked_up = sizes[t][:].indirect(n2_list[:, s0 // 16 : (s0 + n) // 16])
             nc.vector.tensor_tensor(both[:], looked_up, firsts[(c, t)][:], ALU.add)
             sums[(c, t)] = both
 
@@ -180,12 +192,12 @@ def tile_picked_pqdiv_none_p_kernel(
             )
             return z
 
-        def second_product(z, s0, n, last):
+        def second_product(z, s0, n, banks, last):
             z_words = keep.tile([P, n], U32, name="z_words%d" % s0, align_bytes=64)
             z_bytes = keep.tile([P, n], U8, name="z_bytes%d" % s0, align_bytes=64)
             nc.vector.quantize_mx(out=z_words[:].bitcast(FP8X4), scales=z_bytes[:], in_=z[:])
             for b in range(2):
-                bank = psum.tile([P, 2 * n], F32, name="out_bank%d_%d" % (s0, b), tag="out_bank", bufs=4)
+                bank = psum.tile([P, 2 * n], F32, name="out_bank%d_%d" % (s0, b), tag="bank%d" % (banks + b))
                 for j in range(2):
                     cols = slice(P * (2 * b + j), P * (2 * b + j + 1))
                     nc.tensor.matmul_mx(
@@ -213,24 +225,26 @@ def tile_picked_pqdiv_none_p_kernel(
         def at(i):
             return steps[i : i + 1] if i >= 0 else []
 
-        take_size(0, halves[-1])
-        for i in range(len(steps) + 3):
+        for tokens in halves:
+            take_size(0, tokens)
+        for i in range(len(steps) + 4):
             if i + 1 < PACK:
-                take_size(i + 1, halves[-1])
-            for c, t in at(i - 2):
+                for tokens in halves:
+                    take_size(i + 1, tokens)
+            for c, t in at(i - 3):
                 take_root(c, t)
             for c, t in at(i):
                 look_up_first(c, t)
-            for c, t in at(i - 3):
+            for c, t in at(i - 4):
                 weigh(c, t)
-            if i == PACK + 3:
-                second_product(first_z, 0, S // 2, False)
+            if i == PACK - 1 + 6:
+                second_product(first_z, 0, S // 2, 0, False)
             for c, t in at(i - 1):
                 look_up_second(c, t)
-            if i == PACK + 2:
+            if i == PACK - 1 + 4:
                 first_z = weave(0, 0, S // 2)
         quarter = S // 4
         third_z = weave(1, 0, quarter)
         fourth_z = weave(1, quarter, 2 * quarter)
-        second_product(third_z, 2 * quarter, quarter, False)
-        second_product(fourth_z, 3 * quarter, quarter, True)
+        second_product(third_z, 2 * quarter, quarter, 2, False)
+        second_product(fourth_z, 3 * quarter, quarter, 4, True)

@@ -19,7 +19,7 @@ P = 128
 PACK = 4
 CHUNKS = ((0, 256), (256, 256))
 VECTOR_LOOKS_UP_BOTH = ((0, 1),)
-SCALAR_LOOKS_UP_BOTH = ((1, 2), (1, 3))
+SCALAR_LOOKS_UP_BOTH = ()
 
 
 def tile_picked_pqdiv_none_p_kernel(
@@ -134,7 +134,7 @@ def tile_picked_pqdiv_none_p_kernel(
 
         out_view = out.rearrange("(m p) n -> p m n", p=P)
         roots = [keep.tile([P, PACK * n], F32, name="roots%d" % c, align_bytes=64) for c, (s0, n) in enumerate(CHUNKS)]
-        half_way = [keep.tile([P, PACK * n], F32, name="half_way%d" % c, align_bytes=64) for c, (s0, n) in enumerate(CHUNKS)]
+        half_way = [keep.tile([P, PACK * n], (F32, BF16)[c], name="half_way%d" % c, align_bytes=64) for c, (s0, n) in enumerate(CHUNKS)]
         sums = {}
 
         firsts = {}
@@ -167,7 +167,12 @@ def tile_picked_pqdiv_none_p_kernel(
         def take_root(c, t):
             s0, n = CHUNKS[c]
             plane = slice(t * n, (t + 1) * n)
-            nc.scalar.activation(roots[c][:, plane], sums[(c, t)][:], ACT.Abs_reciprocal_sqrt, bias=8.0, scale=16.0)
+            if c == 0:
+                nc.scalar.activation(roots[c][:, plane], sums[(c, t)][:], ACT.Abs_reciprocal_sqrt, bias=8.0, scale=16.0)
+            else:
+                root = keep.tile([P, n], F32, name="root%d" % t, align_bytes=64)
+                nc.scalar.activation(root[:], sums[(c, t)][:], ACT.Abs_reciprocal_sqrt, bias=8.0, scale=16.0)
+                nc.scalar.activation(roots[c][:, plane], root[:], ACT.Square)
 
         def weigh(c, t):
             s0, n = CHUNKS[c]
@@ -184,12 +189,18 @@ def tile_picked_pqdiv_none_p_kernel(
         def weave(c, lo, hi):
             n = CHUNKS[c][1]
             z = keep.tile([P, PACK * (hi - lo)], BF16, name="z%d_%d" % (c, lo), align_bytes=64)
-            nc.vector.tensor_tensor(
-                z[:].rearrange("p (c i t) -> p c t i", i=4, t=PACK),
-                half_way[c][:].rearrange("p (t n) -> p t n", t=PACK)[:, :, lo:hi].rearrange("p t (c i) -> p c t i", i=4),
-                roots[c][:].rearrange("p (t n) -> p t n", t=PACK)[:, :, lo:hi].rearrange("p t (c i) -> p c t i", i=4),
-                ALU.mult,
-            )
+            if c == 0:
+                nc.vector.tensor_tensor(
+                    z[:].rearrange("p (c i t) -> p c t i", i=2, t=PACK),
+                    half_way[c][:].rearrange("p (t c i) -> p c t i", i=2, t=PACK),
+                    roots[c][:].rearrange("p (t c i) -> p c t i", i=2, t=PACK),
+                    ALU.mult,
+                )
+            else:
+                nc.vector.tensor_copy(
+                    z[:].rearrange("p (c i t) -> p c t i", i=4, t=PACK),
+                    half_way[c][:].rearrange("p (t n) -> p t n", t=PACK)[:, :, lo:hi].rearrange("p t (c i) -> p c t i", i=4),
+                )
             return z
 
         def second_product(z, s0, n, banks, last):
@@ -227,7 +238,7 @@ def tile_picked_pqdiv_none_p_kernel(
 
         for tokens in halves:
             take_size(0, tokens)
-        for i in range(len(steps) + 4):
+        for i in range(len(steps) + 5):
             if i + 1 < PACK:
                 for tokens in halves:
                     take_size(i + 1, tokens)
@@ -235,13 +246,13 @@ def tile_picked_pqdiv_none_p_kernel(
                 take_root(c, t)
             for c, t in at(i):
                 look_up_first(c, t)
-            for c, t in at(i - 4):
+            for c, t in at(i - 5):
                 weigh(c, t)
             if i == PACK - 1 + 6:
                 second_product(first_z, 0, S // 2, 0, False)
             for c, t in at(i - 1):
                 look_up_second(c, t)
-            if i == PACK - 1 + 4:
+            if i == PACK - 1 + 5:
                 first_z = weave(0, 0, S // 2)
         quarter = S // 4
         third_z = weave(1, 0, quarter)

@@ -2,7 +2,7 @@ from contextlib import ExitStack
 
 import concourse.mybir as mybir
 
-K, T, S, G, H = 512, 2048, 512, 2048, 512
+K, T, S, H = 512, 2048, 512, 512
 FLOPS = 2 * 2 * K * H * S
 
 F32 = mybir.dt.float32
@@ -16,10 +16,18 @@ ACT = mybir.ActivationFunctionType
 ALU = mybir.AluOpType
 
 P = 128
-PACK = 4
-CHUNKS = ((0, 256), (256, 256))
-VECTOR_LOOKS_UP_BOTH = ((0, 1),)
-SCALAR_LOOKS_UP_BOTH = ()
+SLOTS = 4
+HALF = S // 2
+QUARTER = S // 4
+SIXTEENTH = 0.0625
+
+ADD_LAG = 1
+ROOT_LAG = 3
+WEIGH_LAG = 5
+RING = 3
+VECTOR_LOOKS_UP_N1 = (0, 1)
+LAST_STEP = (1, SLOTS - 1)
+VECTOR_ZEROES = 352
 
 
 def tile_picked_pqdiv_none_p_kernel(
@@ -35,227 +43,223 @@ def tile_picked_pqdiv_none_p_kernel(
             nc.sync.dma_start(tile[:], src)
             return tile
 
-        def load_words(name, src, pieces):
+        def load_words(name, src, loads):
             tile = keep.tile([P, T], I32, name=name, align_bytes=64)
             words = src[0].rearrange("p c r -> p (c r)").bitcast(I32)
-            for piece in range(pieces):
-                cols = slice(piece * T // pieces, (piece + 1) * T // pieces)
+            for i in range(loads):
+                cols = slice(i * T // loads, (i + 1) * T // loads)
                 nc.sync.dma_start(tile[:, cols], words[:, cols])
             return tile
 
-        def gather(name, table, dtype, offsets, tag):
+        def entries(list_tile, tokens):
+            return list_tile[:, tokens.start // 16 : tokens.stop // 16]
+
+        def gather(name, table, dtype, list_tile, tag):
             tile = keep.tile([P, S], dtype, name=name, tag=tag, align_bytes=64)
-            nc.vector.tensor_copy(tile[:], table[:].bitcast(dtype).indirect(offsets[:]))
+            nc.vector.tensor_copy(tile[:], table[:].bitcast(dtype).indirect(list_tile[:]))
             return tile
 
-        def rows_to_places(plane, source, rows):
+        def move_scale_rows(target, source, rows, queues):
             for a in rows:
-                nc.sync.dma_start(plane[:].bitcast(I32)[a:P:32, :], source[:].bitcast(I32)[8 * a : P : 32, :])
+                queues[a % len(queues)].dma_start(
+                    target[:].bitcast(I32)[a:P:32, :], source[:].bitcast(I32)[8 * a : P : 32, :]
+                )
 
-        d_bytes_all = keep.tile([P, G // 4], I32, name="d_bytes_all", align_bytes=64)
+        d_bytes_all = keep.tile([P, T // 4], I32, name="d_bytes_all", align_bytes=64)
         x_bytes_all = keep.tile([P, T // 4], I32, name="x_bytes_all", align_bytes=64)
-        nc.vector.memset(d_bytes_all[:], 0)
-        nc.vector.memset(x_bytes_all[:, 0 : T // 8], 0)
-        nc.gpsimd.memset(x_bytes_all[:, T // 8 : T // 4], 0)
+        for table in (d_bytes_all, x_bytes_all):
+            nc.vector.memset(table[:, 0:VECTOR_ZEROES], 0)
+            nc.gpsimd.memset(table[:, VECTOR_ZEROES : T // 4], 0)
         k1_list = load_list("k1_list", k1)
         offs_list = load_list("offs_list", offs)
         nc.sync.dma_start(d_bytes_all[0:P:8, :], d_scales[0].bitcast(I32))
         nc.sync.dma_start(x_bytes_all[0:P:8, :], x_scales[0].bitcast(I32))
         d_words_all = load_words("d_words_all", d_words, 1)
         x_words_all = load_words("x_words_all", x_words, 2)
-        gs_sb = keep.tile([P, PACK], F32, name="gs_sb")
-        nc.sync.dma_start(gs_sb[:], gs.rearrange("(p t) o -> p (t o)", t=PACK))
+        gs_sb = keep.tile([P, SLOTS], F32, name="gs_sb")
+        nc.sync.dma_start(gs_sb[:], gs.rearrange("(p t) o -> p (t o)", t=SLOTS))
         n1_list = load_list("n1_list", n1)
         n2_list = load_list("n2_list", n2)
 
         warm_in = keep.tile([P, 1], F32, name="warm_in")
         nc.gpsimd.memset(warm_in[:], 1.0)
-        warm = keep.tile([P, 1], F32, name="warm")
-        nc.scalar.activation(warm[:], warm_in[:], ACT.Abs_reciprocal_sqrt)
+        warm_out = keep.tile([P, 1], F32, name="warm_out")
+        nc.scalar.activation(warm_out[:], warm_in[:], ACT.Abs_reciprocal_sqrt)
 
-        first_plane = keep.tile([P, H + S], U8, name="first_plane", align_bytes=64)
+        first_scales = keep.tile([P, H + S], U8, name="first_scales", align_bytes=64)
         w1_bytes = gather("w1_bytes", d_bytes_all, U8, k1_list, "w1")
         x_bytes = gather("x_bytes", x_bytes_all, U8, offs_list, "x")
         nc.vector.tensor_copy(
-            first_plane[:, 0:H].rearrange("p (t m) -> p t m", t=PACK),
-            w1_bytes[:].rearrange("p (m t) -> p t m", t=PACK),
+            first_scales[:, 0:H].rearrange("p (t m) -> p t m", t=SLOTS),
+            w1_bytes[:].rearrange("p (m t) -> p t m", t=SLOTS),
         )
-        nc.vector.tensor_copy(first_plane[:, H : H + S].bitcast(I32), x_bytes[:].bitcast(I32))
-        rows_to_places(first_plane, first_plane, range(1, 4))
+        nc.vector.tensor_copy(first_scales[:, H : H + S].bitcast(I32), x_bytes[:].bitcast(I32))
+        move_scale_rows(first_scales, first_scales, range(1, 4), (nc.scalar, nc.sync))
         k2_list = load_list("k2_list", k2)
+
         w1_picked = gather("w1_picked", d_words_all, U32, k1_list, "w1")
         w1_dealt = keep.tile([P, H], U32, name="w1_dealt", align_bytes=64)
-        nc.vector.tensor_copy(
-            w1_dealt[:].rearrange("p (t c i) -> p c t i", t=PACK, i=4),
-            w1_picked[:].rearrange("p (c i t) -> p c t i", t=PACK, i=4),
-        )
         x_picked = keep.tile([P, S], U32, name="x_picked", tag="x", align_bytes=64)
         h_banks = [
-            [psum.tile([P, S // 2], F32, name="h_bank%d_%d" % (half, t), tag="bank%d" % (PACK * half + t)) for t in range(PACK)]
+            [psum.tile([P, HALF], F32, name="h%d_%d" % (half, t), tag="bank%d" % (SLOTS * half + t)) for t in range(SLOTS)]
             for half in range(2)
         ]
+        sizes = [keep.tile([P, S], F32, name="size%d" % t, align_bytes=64) for t in range(SLOTS)]
+        halves = (slice(0, HALF), slice(HALF, S))
 
-        def h_raw(t, tokens):
-            half, start = divmod(tokens.start, S // 2)
-            return h_banks[half][t][:, start : start + tokens.stop - tokens.start]
-
-        sizes = [keep.tile([P, S], F32, name="size%d" % t, align_bytes=64) for t in range(PACK)]
-
-        def first_product(t, tokens):
-            cols = slice(P * t, P * (t + 1))
-            nc.tensor.matmul_mx(
-                out=h_raw(t, tokens),
-                lhsT=w1_dealt[:, cols].bitcast(FP8X4),
-                lhsT_scale=first_plane[:, cols],
-                rhs=x_picked[:, tokens].bitcast(FP8X4),
-                rhs_scale=first_plane[:, H + tokens.start : H + tokens.stop],
-                start=True,
-                stop=True,
-            )
-
-        def take_size(t, tokens):
-            nc.scalar.activation(sizes[t][:, tokens], h_raw(t, tokens), ACT.Abs, scale=0.0625)
-
-        halves = (slice(0, S // 2), slice(S // 2, S))
-        for tokens in halves:
+        def gather_x(tokens):
             nc.vector.tensor_copy(
-                x_picked[:, tokens],
-                x_words_all[:].bitcast(U32).indirect(offs_list[:, tokens.start // 16 : tokens.stop // 16]),
+                x_picked[:, tokens], x_words_all[:].bitcast(U32).indirect(entries(offs_list, tokens))
             )
-        for pair in range(2):
-            for tokens in halves:
-                for t in (2 * pair, 2 * pair + 1):
-                    first_product(t, tokens)
+
+        gather_x(halves[0])
+        nc.vector.tensor_copy(
+            w1_dealt[:].rearrange("p (t c i) -> p c t i", t=SLOTS, i=4),
+            w1_picked[:].rearrange("p (c i t) -> p c t i", t=SLOTS, i=4),
+        )
+        gather_x(halves[1])
+
+        for pair in ((0, 1), (2, 3)):
+            for half, tokens in enumerate(halves):
+                for t in pair:
+                    cols = slice(P * t, P * (t + 1))
+                    nc.tensor.matmul_mx(
+                        out=h_banks[half][t][:],
+                        lhsT=w1_dealt[:, cols].bitcast(FP8X4),
+                        lhsT_scale=first_scales[:, cols],
+                        rhs=x_picked[:, tokens].bitcast(FP8X4),
+                        rhs_scale=first_scales[:, H + tokens.start : H + tokens.stop],
+                        start=True,
+                        stop=True,
+                    )
 
         w2_bytes = gather("w2_bytes", d_bytes_all, U8, k2_list, "w1")
-        second_plane = keep.tile([P, H], U8, name="second_plane", align_bytes=64)
-        rows_to_places(second_plane, w2_bytes, range(4))
+        w2_scales = keep.tile([P, H], U8, name="w2_scales", align_bytes=64)
+        move_scale_rows(w2_scales, w2_bytes, range(4), (nc.sync,))
         w2_picked = gather("w2_picked", d_words_all, U32, k2_list, "w2_picked")
 
         out_view = out.rearrange("(m p) n -> p m n", p=P)
-        roots = [keep.tile([P, PACK * n], F32, name="roots%d" % c, align_bytes=64) for c, (s0, n) in enumerate(CHUNKS)]
-        half_way = [keep.tile([P, PACK * n], (F32, BF16)[c], name="half_way%d" % c, align_bytes=64) for c, (s0, n) in enumerate(CHUNKS)]
+        factors = [keep.tile([P, SLOTS * HALF], F32, name="factors%d" % half, align_bytes=64) for half in range(2)]
+        weighed = [
+            keep.tile([P, SLOTS * HALF], dtype, name="weighed%d" % half, align_bytes=64)
+            for half, dtype in enumerate((F32, BF16))
+        ]
+        by_n1 = {}
         sums = {}
 
-        firsts = {}
-        seconds = {}
+        def take_size(t):
+            for half, tokens in enumerate(halves):
+                nc.scalar.activation(sizes[t][:, tokens], h_banks[half][t][:], ACT.Abs, scale=SIXTEENTH)
 
-        def look_up_first(c, t):
-            s0, n = CHUNKS[c]
-            first = keep.tile([P, n], F32, name="first%d_%d" % (c, t), tag="first", bufs=3, align_bytes=64)
-            looked_up = sizes[t][:].indirect(n1_list[:, s0 // 16 : (s0 + n) // 16])
-            if (c, t) in VECTOR_LOOKS_UP_BOTH:
-                nc.vector.tensor_copy(first[:], looked_up)
+        def look_up_n1(half, t):
+            tile = keep.tile([P, HALF], F32, name="by_n1_%d_%d" % (half, t), tag="by_n1", bufs=RING, align_bytes=64)
+            looked_up = sizes[t][:].indirect(entries(n1_list, halves[half]))
+            if (half, t) == VECTOR_LOOKS_UP_N1:
+                nc.vector.tensor_copy(tile[:], looked_up)
             else:
-                nc.scalar.activation(first[:], looked_up, ACT.Copy)
-            if (c, t) in SCALAR_LOOKS_UP_BOTH:
-                second = keep.tile([P, n], F32, name="second%d_%d" % (c, t), align_bytes=64)
-                nc.scalar.activation(second[:], sizes[t][:].indirect(n2_list[:, s0 // 16 : (s0 + n) // 16]), ACT.Copy)
-                seconds[(c, t)] = second
-            firsts[(c, t)] = first
+                nc.scalar.activation(tile[:], looked_up, ACT.Copy)
+            by_n1[(half, t)] = tile
 
-        def look_up_second(c, t):
-            s0, n = CHUNKS[c]
-            both = keep.tile([P, n], F32, name="both%d_%d" % (c, t), tag="both", bufs=3, align_bytes=64)
-            if (c, t) in SCALAR_LOOKS_UP_BOTH:
-                looked_up = seconds[(c, t)][:]
-            else:
-                looked_up = sizes[t][:].indirect(n2_list[:, s0 // 16 : (s0 + n) // 16])
-            nc.vector.tensor_tensor(both[:], looked_up, firsts[(c, t)][:], ALU.add)
-            sums[(c, t)] = both
+        def look_up_n2_and_add(half, t):
+            tile = keep.tile([P, HALF], F32, name="sum%d_%d" % (half, t), tag="sum", bufs=RING, align_bytes=64)
+            looked_up = sizes[t][:].indirect(entries(n2_list, halves[half]))
+            nc.vector.tensor_tensor(tile[:], looked_up, by_n1[(half, t)][:], ALU.add)
+            sums[(half, t)] = tile
 
-        def take_root(c, t):
-            s0, n = CHUNKS[c]
-            plane = slice(t * n, (t + 1) * n)
-            if c == 0:
-                nc.scalar.activation(roots[c][:, plane], sums[(c, t)][:], ACT.Abs_reciprocal_sqrt, bias=8.0, scale=16.0)
-            else:
-                root = keep.tile([P, n], F32, name="root%d" % t, align_bytes=64)
-                nc.scalar.activation(root[:], sums[(c, t)][:], ACT.Abs_reciprocal_sqrt, bias=8.0, scale=16.0)
-                nc.scalar.activation(roots[c][:, plane], root[:], ACT.Square)
+        def pieces(half, t):
+            return ((0, QUARTER), (QUARTER, HALF)) if (half, t) == LAST_STEP else ((0, HALF),)
 
-        def weigh(c, t):
-            s0, n = CHUNKS[c]
-            plane = slice(t * n, (t + 1) * n)
-            nc.vector.scalar_tensor_tensor(
-                half_way[c][:, plane],
-                h_raw(t, slice(s0, s0 + n)),
-                gs_sb[:, t : t + 1],
-                roots[c][:, plane],
-                ALU.mult,
-                ALU.mult,
-            )
+        def take_root(half, t):
+            for lo, hi in pieces(half, t):
+                factor = factors[half][:, t * HALF + lo : t * HALF + hi]
+                total = sums[(half, t)][:, lo:hi]
+                if half == 0:
+                    nc.scalar.activation(factor, total, ACT.Abs_reciprocal_sqrt, bias=8.0, scale=16.0)
+                else:
+                    root = keep.tile([P, hi - lo], F32, name="root%d_%d" % (t, lo), align_bytes=64)
+                    nc.scalar.activation(root[:], total, ACT.Abs_reciprocal_sqrt, bias=8.0, scale=16.0)
+                    nc.scalar.activation(factor, root[:], ACT.Square)
 
-        def weave(c, lo, hi):
-            n = CHUNKS[c][1]
-            z = keep.tile([P, PACK * (hi - lo)], BF16, name="z%d_%d" % (c, lo), align_bytes=64)
-            if c == 0:
-                nc.vector.tensor_tensor(
-                    z[:].rearrange("p (c i t) -> p c t i", i=2, t=PACK),
-                    half_way[c][:].rearrange("p (t c i) -> p c t i", i=2, t=PACK),
-                    roots[c][:].rearrange("p (t c i) -> p c t i", i=2, t=PACK),
+        def weigh(half, t):
+            for lo, hi in pieces(half, t):
+                cols = slice(t * HALF + lo, t * HALF + hi)
+                nc.vector.scalar_tensor_tensor(
+                    weighed[half][:, cols],
+                    h_banks[half][t][:, lo:hi],
+                    gs_sb[:, t : t + 1],
+                    factors[half][:, cols],
+                    ALU.mult,
                     ALU.mult,
                 )
-            else:
-                nc.vector.tensor_copy(
-                    z[:].rearrange("p (c i t) -> p c t i", i=4, t=PACK),
-                    half_way[c][:].rearrange("p (t n) -> p t n", t=PACK)[:, :, lo:hi].rearrange("p t (c i) -> p c t i", i=4),
-                )
+
+        def weave_first_half():
+            z = keep.tile([P, SLOTS * HALF], BF16, name="z_first", align_bytes=64)
+            nc.vector.tensor_tensor(
+                z[:].rearrange("p (c i t) -> p c t i", i=2, t=SLOTS),
+                weighed[0][:].rearrange("p (t c i) -> p c t i", i=2, t=SLOTS),
+                factors[0][:].rearrange("p (t c i) -> p c t i", i=2, t=SLOTS),
+                ALU.mult,
+            )
             return z
 
-        def second_product(z, s0, n, banks, last):
-            z_words = keep.tile([P, n], U32, name="z_words%d" % s0, align_bytes=64)
-            z_bytes = keep.tile([P, n], U8, name="z_bytes%d" % s0, align_bytes=64)
-            nc.vector.quantize_mx(out=z_words[:].bitcast(FP8X4), scales=z_bytes[:], in_=z[:])
+        def weave_quarter(lo):
+            z = keep.tile([P, SLOTS * QUARTER], BF16, name="z_quarter%d" % lo, align_bytes=64)
+            slots = weighed[1][:].rearrange("p (t n) -> p t n", t=SLOTS)[:, :, lo : lo + QUARTER]
+            nc.vector.tensor_copy(
+                z[:].rearrange("p (c i t) -> p c t i", i=4, t=SLOTS),
+                slots.rearrange("p t (c i) -> p c t i", i=4),
+            )
+            return z
+
+        def second_product(z, tokens, first_bank, last):
+            n = tokens.stop - tokens.start
+            z_words = keep.tile([P, n], U32, name="z_words%d" % tokens.start, align_bytes=64)
+            z_scales = keep.tile([P, n], U8, name="z_scales%d" % tokens.start, align_bytes=64)
+            nc.vector.quantize_mx(out=z_words[:].bitcast(FP8X4), scales=z_scales[:], in_=z[:])
             for b in range(2):
-                bank = psum.tile([P, 2 * n], F32, name="out_bank%d_%d" % (s0, b), tag="bank%d" % (banks + b))
+                bank = psum.tile([P, 2 * n], F32, name="out%d_%d" % (tokens.start, b), tag="bank%d" % (first_bank + b))
                 for j in range(2):
                     cols = slice(P * (2 * b + j), P * (2 * b + j + 1))
                     nc.tensor.matmul_mx(
                         out=bank[:, j * n : (j + 1) * n],
                         lhsT=w2_picked[:, cols].bitcast(FP8X4),
-                        lhsT_scale=second_plane[:, cols],
+                        lhsT_scale=w2_scales[:, cols],
                         rhs=z_words[:].bitcast(FP8X4),
-                        rhs_scale=z_bytes[:],
+                        rhs_scale=z_scales[:],
                         start=True,
                         stop=True,
                     )
-                result = keep.tile([P, 2 * n], F32, name="result%d_%d" % (s0, b), align_bytes=64)
-                if b == 1 and last:
-                    nc.vector.tensor_scalar_mul(result[:], bank[:], 0.0625)
+                result = keep.tile([P, 2 * n], F32, name="result%d_%d" % (tokens.start, b), align_bytes=64)
+                if last and b == 1:
+                    nc.vector.tensor_scalar_mul(result[:], bank[:], SIXTEENTH)
                 else:
-                    nc.scalar.activation(result[:], bank[:], ACT.Copy, scale=0.0625)
-                queue = nc.scalar if b == 0 and last else nc.sync
+                    nc.scalar.activation(result[:], bank[:], ACT.Copy, scale=SIXTEENTH)
+                queue = nc.scalar if last and b == 0 else nc.sync
                 queue.dma_start(
-                    out_view[:, 2 * b : 2 * b + 2, s0 : s0 + n],
+                    out_view[:, 2 * b : 2 * b + 2, tokens],
                     result[:].rearrange("p (j n) -> p j n", j=2),
                 )
 
-        steps = [(c, t) for c in range(len(CHUNKS)) for t in range(PACK)]
+        steps = [(half, t) for half in range(2) for t in range(SLOTS)]
 
-        def at(i):
-            return steps[i : i + 1] if i >= 0 else []
+        def stage(work, i):
+            if 0 <= i < len(steps):
+                work(*steps[i])
 
-        for tokens in halves:
-            take_size(0, tokens)
-        for i in range(len(steps) + 5):
-            if i + 1 < PACK:
-                for tokens in halves:
-                    take_size(i + 1, tokens)
-            for c, t in at(i - 3):
-                take_root(c, t)
-            for c, t in at(i):
-                look_up_first(c, t)
-            for c, t in at(i - 5):
-                weigh(c, t)
-            if i == PACK - 1 + 6:
-                second_product(first_z, 0, S // 2, 0, False)
-            for c, t in at(i - 1):
-                look_up_second(c, t)
-            if i == PACK - 1 + 5:
-                first_z = weave(0, 0, S // 2)
-        quarter = S // 4
-        third_z = weave(1, 0, quarter)
-        fourth_z = weave(1, quarter, 2 * quarter)
-        second_product(third_z, 2 * quarter, quarter, 2, False)
-        second_product(fourth_z, 3 * quarter, quarter, 4, True)
+        first_half_weighed = SLOTS - 1 + WEIGH_LAG
+        take_size(0)
+        for i in range(len(steps) + WEIGH_LAG):
+            if i + 1 < SLOTS:
+                take_size(i + 1)
+            stage(take_root, i - ROOT_LAG)
+            stage(look_up_n1, i)
+            stage(weigh, i - WEIGH_LAG)
+            if i == first_half_weighed + 1:
+                second_product(z_first, halves[0], 0, False)
+            stage(look_up_n2_and_add, i - ADD_LAG)
+            if i == first_half_weighed:
+                z_first = weave_first_half()
+        z_third = weave_quarter(0)
+        z_fourth = weave_quarter(QUARTER)
+        second_product(z_third, slice(HALF, HALF + QUARTER), 2, False)
+        second_product(z_fourth, slice(HALF + QUARTER, S), 4, True)

from contextlib import ExitStack

import concourse.mybir as mybir

K, T, S, H = 512, 2048, 512, 512
FLOPS = 2 * 2 * K * H * S

F32 = mybir.dt.float32
BF16 = mybir.dt.bfloat16
I32 = mybir.dt.int32
U32 = mybir.dt.uint32
U16 = mybir.dt.uint16
U8 = mybir.dt.uint8
FP8X4 = mybir.dt.float8_e4m3fn_x4
ACT = mybir.ActivationFunctionType
ALU = mybir.AluOpType

P = 128
SLOTS = 4
HALF = S // 2
QUARTER = S // 4
SIXTEENTH = 0.0625

ADD_LAG = 1
ROOT_LAG = 3
WEIGH_LAG = 5
RING = 3
VECTOR_LOOKS_UP_N1 = (0, 1)
LAST_STEP = (1, SLOTS - 1)
VECTOR_ZEROES = 352


def tile_picked_pqdiv_none_p_kernel(
    tc, x_words, x_scales, d_words, d_scales, gs, offs, k1, n1, n2, k2, out
):
    nc = tc.nc
    with ExitStack() as ctx:
        keep = ctx.enter_context(tc.tile_pool(name="keep", bufs=1))
        psum = ctx.enter_context(tc.psum_pool(name="psum", bufs=1))

        def load_list(name, src):
            tile = keep.tile([P, S // 16], U16, name=name)
            nc.sync.dma_start(tile[:], src)
            return tile

        def load_words(name, src, loads):
            tile = keep.tile([P, T], I32, name=name, align_bytes=64)
            words = src[0].rearrange("p c r -> p (c r)").bitcast(I32)
            for i in range(loads):
                cols = slice(i * T // loads, (i + 1) * T // loads)
                nc.sync.dma_start(tile[:, cols], words[:, cols])
            return tile

        def entries(list_tile, tokens):
            return list_tile[:, tokens.start // 16 : tokens.stop // 16]

        def gather(name, table, dtype, list_tile, tag):
            tile = keep.tile([P, S], dtype, name=name, tag=tag, align_bytes=64)
            nc.vector.tensor_copy(tile[:], table[:].bitcast(dtype).indirect(list_tile[:]))
            return tile

        def move_scale_rows(target, source, rows, queues):
            for a in rows:
                queues[a % len(queues)].dma_start(
                    target[:].bitcast(I32)[a:P:32, :], source[:].bitcast(I32)[8 * a : P : 32, :]
                )

        d_bytes_all = keep.tile([P, T // 4], I32, name="d_bytes_all", align_bytes=64)
        x_bytes_all = keep.tile([P, T // 4], I32, name="x_bytes_all", align_bytes=64)
        for table in (d_bytes_all, x_bytes_all):
            nc.vector.memset(table[:, 0:VECTOR_ZEROES], 0)
            nc.gpsimd.memset(table[:, VECTOR_ZEROES : T // 4], 0)
        k1_list = load_list("k1_list", k1)
        offs_list = load_list("offs_list", offs)
        nc.sync.dma_start(d_bytes_all[0:P:8, :], d_scales[0].bitcast(I32))
        nc.sync.dma_start(x_bytes_all[0:P:8, :], x_scales[0].bitcast(I32))
        d_words_all = load_words("d_words_all", d_words, 1)
        x_words_all = load_words("x_words_all", x_words, 2)
        gs_sb = keep.tile([P, SLOTS], F32, name="gs_sb")
        nc.sync.dma_start(gs_sb[:], gs.rearrange("(p t) o -> p (t o)", t=SLOTS))
        n1_list = load_list("n1_list", n1)
        n2_list = load_list("n2_list", n2)

        warm_in = keep.tile([P, 1], F32, name="warm_in")
        nc.gpsimd.memset(warm_in[:], 1.0)
        warm_out = keep.tile([P, 1], F32, name="warm_out")
        nc.scalar.activation(warm_out[:], warm_in[:], ACT.Abs_reciprocal_sqrt)

        first_scales = keep.tile([P, H + S], U8, name="first_scales", align_bytes=64)
        w1_bytes = gather("w1_bytes", d_bytes_all, U8, k1_list, "w1")
        x_bytes = gather("x_bytes", x_bytes_all, U8, offs_list, "x")
        nc.vector.tensor_copy(
            first_scales[:, 0:H].rearrange("p (t m) -> p t m", t=SLOTS),
            w1_bytes[:].rearrange("p (m t) -> p t m", t=SLOTS),
        )
        nc.vector.tensor_copy(first_scales[:, H : H + S].bitcast(I32), x_bytes[:].bitcast(I32))
        move_scale_rows(first_scales, first_scales, range(1, 4), (nc.scalar, nc.sync))
        k2_list = load_list("k2_list", k2)

        w1_picked = gather("w1_picked", d_words_all, U32, k1_list, "w1")
        w1_dealt = keep.tile([P, H], U32, name="w1_dealt", align_bytes=64)
        x_picked = keep.tile([P, S], U32, name="x_picked", tag="x", align_bytes=64)
        h_banks = [
            [psum.tile([P, HALF], F32, name="h%d_%d" % (half, t), tag="bank%d" % (SLOTS * half + t)) for t in range(SLOTS)]
            for half in range(2)
        ]
        sizes = [keep.tile([P, S], F32, name="size%d" % t, align_bytes=64) for t in range(SLOTS)]
        halves = (slice(0, HALF), slice(HALF, S))

        def gather_x(tokens):
            nc.vector.tensor_copy(
                x_picked[:, tokens], x_words_all[:].bitcast(U32).indirect(entries(offs_list, tokens))
            )

        gather_x(halves[0])
        nc.vector.tensor_copy(
            w1_dealt[:].rearrange("p (t c i) -> p c t i", t=SLOTS, i=4),
            w1_picked[:].rearrange("p (c i t) -> p c t i", t=SLOTS, i=4),
        )
        gather_x(halves[1])

        for pair in ((0, 1), (2, 3)):
            for half, tokens in enumerate(halves):
                for t in pair:
                    cols = slice(P * t, P * (t + 1))
                    nc.tensor.matmul_mx(
                        out=h_banks[half][t][:],
                        lhsT=w1_dealt[:, cols].bitcast(FP8X4),
                        lhsT_scale=first_scales[:, cols],
                        rhs=x_picked[:, tokens].bitcast(FP8X4),
                        rhs_scale=first_scales[:, H + tokens.start : H + tokens.stop],
                        start=True,
                        stop=True,
                    )

        w2_bytes = gather("w2_bytes", d_bytes_all, U8, k2_list, "w1")
        w2_scales = keep.tile([P, H], U8, name="w2_scales", align_bytes=64)
        move_scale_rows(w2_scales, w2_bytes, range(4), (nc.sync,))
        w2_picked = gather("w2_picked", d_words_all, U32, k2_list, "w2_picked")

        out_view = out.rearrange("(m p) n -> p m n", p=P)
        factors = [keep.tile([P, SLOTS * HALF], F32, name="factors%d" % half, align_bytes=64) for half in range(2)]
        weighed = [
            keep.tile([P, SLOTS * HALF], dtype, name="weighed%d" % half, align_bytes=64)
            for half, dtype in enumerate((F32, BF16))
        ]
        by_n1 = {}
        sums = {}

        def take_size(t):
            for half, tokens in enumerate(halves):
                nc.scalar.activation(sizes[t][:, tokens], h_banks[half][t][:], ACT.Abs, scale=SIXTEENTH)

        def look_up_n1(half, t):
            tile = keep.tile([P, HALF], F32, name="by_n1_%d_%d" % (half, t), tag="by_n1", bufs=RING, align_bytes=64)
            looked_up = sizes[t][:].indirect(entries(n1_list, halves[half]))
            if (half, t) == VECTOR_LOOKS_UP_N1:
                nc.vector.tensor_copy(tile[:], looked_up)
            else:
                nc.scalar.activation(tile[:], looked_up, ACT.Copy)
            by_n1[(half, t)] = tile

        def look_up_n2_and_add(half, t):
            tile = keep.tile([P, HALF], F32, name="sum%d_%d" % (half, t), tag="sum", bufs=RING, align_bytes=64)
            looked_up = sizes[t][:].indirect(entries(n2_list, halves[half]))
            nc.vector.tensor_tensor(tile[:], looked_up, by_n1[(half, t)][:], ALU.add)
            sums[(half, t)] = tile

        def pieces(half, t):
            return ((0, QUARTER), (QUARTER, HALF)) if (half, t) == LAST_STEP else ((0, HALF),)

        def take_root(half, t):
            for lo, hi in pieces(half, t):
                factor = factors[half][:, t * HALF + lo : t * HALF + hi]
                total = sums[(half, t)][:, lo:hi]
                if half == 0:
                    nc.scalar.activation(factor, total, ACT.Abs_reciprocal_sqrt, bias=8.0, scale=16.0)
                else:
                    root = keep.tile([P, hi - lo], F32, name="root%d_%d" % (t, lo), align_bytes=64)
                    nc.scalar.activation(root[:], total, ACT.Abs_reciprocal_sqrt, bias=8.0, scale=16.0)
                    nc.scalar.activation(factor, root[:], ACT.Square)

        def weigh(half, t):
            for lo, hi in pieces(half, t):
                cols = slice(t * HALF + lo, t * HALF + hi)
                nc.vector.scalar_tensor_tensor(
                    weighed[half][:, cols],
                    h_banks[half][t][:, lo:hi],
                    gs_sb[:, t : t + 1],
                    factors[half][:, cols],
                    ALU.mult,
                    ALU.mult,
                )

        def weave_first_half():
            z = keep.tile([P, SLOTS * HALF], BF16, name="z_first", align_bytes=64)
            nc.vector.tensor_tensor(
                z[:].rearrange("p (c i t) -> p c t i", i=2, t=SLOTS),
                weighed[0][:].rearrange("p (t c i) -> p c t i", i=2, t=SLOTS),
                factors[0][:].rearrange("p (t c i) -> p c t i", i=2, t=SLOTS),
                ALU.mult,
            )
            return z

        def weave_quarter(lo):
            z = keep.tile([P, SLOTS * QUARTER], BF16, name="z_quarter%d" % lo, align_bytes=64)
            slots = weighed[1][:].rearrange("p (t n) -> p t n", t=SLOTS)[:, :, lo : lo + QUARTER]
            nc.vector.tensor_copy(
                z[:].rearrange("p (c i t) -> p c t i", i=4, t=SLOTS),
                slots.rearrange("p t (c i) -> p c t i", i=4),
            )
            return z

        def second_product(z, tokens, first_bank, last):
            n = tokens.stop - tokens.start
            z_words = keep.tile([P, n], U32, name="z_words%d" % tokens.start, align_bytes=64)
            z_scales = keep.tile([P, n], U8, name="z_scales%d" % tokens.start, align_bytes=64)
            nc.vector.quantize_mx(out=z_words[:].bitcast(FP8X4), scales=z_scales[:], in_=z[:])
            for b in range(2):
                bank = psum.tile([P, 2 * n], F32, name="out%d_%d" % (tokens.start, b), tag="bank%d" % (first_bank + b))
                for j in range(2):
                    cols = slice(P * (2 * b + j), P * (2 * b + j + 1))
                    nc.tensor.matmul_mx(
                        out=bank[:, j * n : (j + 1) * n],
                        lhsT=w2_picked[:, cols].bitcast(FP8X4),
                        lhsT_scale=w2_scales[:, cols],
                        rhs=z_words[:].bitcast(FP8X4),
                        rhs_scale=z_scales[:],
                        start=True,
                        stop=True,
                    )
                result = keep.tile([P, 2 * n], F32, name="result%d_%d" % (tokens.start, b), align_bytes=64)
                if last and b == 1:
                    nc.vector.tensor_scalar_mul(result[:], bank[:], SIXTEENTH)
                else:
                    nc.scalar.activation(result[:], bank[:], ACT.Copy, scale=SIXTEENTH)
                queue = nc.scalar if last and b == 0 else nc.sync
                queue.dma_start(
                    out_view[:, 2 * b : 2 * b + 2, tokens],
                    result[:].rearrange("p (j n) -> p j n", j=2),
                )

        steps = [(half, t) for half in range(2) for t in range(SLOTS)]

        def stage(work, i):
            if 0 <= i < len(steps):
                work(*steps[i])

        first_half_weighed = SLOTS - 1 + WEIGH_LAG
        take_size(0)
        for i in range(len(steps) + WEIGH_LAG):
            if i + 1 < SLOTS:
                take_size(i + 1)
            stage(take_root, i - ROOT_LAG)
            stage(look_up_n1, i)
            stage(weigh, i - WEIGH_LAG)
            if i == first_half_weighed + 1:
                second_product(z_first, halves[0], 0, False)
            stage(look_up_n2_and_add, i - ADD_LAG)
            if i == first_half_weighed:
                z_first = weave_first_half()
        z_third = weave_quarter(0)
        z_fourth = weave_quarter(QUARTER)
        second_product(z_third, slice(HALF, HALF + QUARTER), 2, False)
        second_product(z_fourth, slice(HALF + QUARTER, S), 4, True)
